import numpy as np
import ml_dtypes


def mxq(x, axis, fmt="e4m3"):
    dtype, down = {"e4m3": (ml_dtypes.float8_e4m3fn, 7), "e5m2": (ml_dtypes.float8_e5m2, 14)}[fmt]
    v = np.moveaxis(np.asarray(x, np.float32).astype(ml_dtypes.bfloat16).astype(np.float64), axis, -1)
    blocks = v.reshape(v.shape[:-1] + (-1, 32))
    amax = np.abs(blocks).max(-1, keepdims=True)
    byte = np.maximum(np.where(amax > 0, np.frexp(amax)[1] - 1 + 127, 0) - down, 1)
    scale = np.exp2(byte - 127.0)
    codes = (blocks / scale).astype(np.float32).astype(dtype).astype(np.float64)
    return np.moveaxis((codes * scale).reshape(v.shape), -1, axis)


WIDE = False


def mx_kscale(k):
    if not WIDE:
        return np.ones(k)
    levels = np.array([10, -10, 5, -5, 0])
    if k % 512:
        return np.exp2(np.random.permutation(np.resize(levels, k // 32))).repeat(32)
    a = np.empty((k // 512, 16))
    for p in range(k // 512):
        a[p, :8] = np.random.permutation(np.resize(levels, 8))
        for g in range(8):
            far = levels[np.abs(levels - a[p, g]) >= 10]
            a[p, g + 8] = far[np.random.randint(len(far))]
    return np.exp2(a.ravel()).repeat(32)


def f64(x):
    return np.asarray(x).astype(np.float64)


def striped(idx):
    return np.tile(idx.reshape(-1, 16).T, (8, 1)).astype(np.uint16)


def unstriped(offs):
    return offs[:16].T.reshape(-1).astype(np.int64)


def pack_weight(w):
    k, n = w.shape
    w = f64(np.asarray(w, np.float32).astype(ml_dtypes.bfloat16)).reshape(k // 32, 32, n)
    amax = np.abs(w).max(1)
    byte = np.clip(np.where(amax > 0, np.frexp(amax)[1] - 1 + 127 - 7, 1), 1, 254)
    scaled = (w * np.exp2(127.0 - byte)[:, None, :]).reshape(k, n).astype(np.float32)
    words = np.ascontiguousarray(scaled.reshape(k // 512, 128, 4, n).transpose(0, 1, 3, 2)).astype(ml_dtypes.float8_e4m3fn).view(np.uint8)
    return words, np.ascontiguousarray(byte.astype(np.uint8).reshape(k // 512, 16, n))


def unpack_weight(words, scales):
    g, p, n, _ = words.shape
    vals = np.ascontiguousarray(words).view(ml_dtypes.float8_e4m3fn).astype(np.float64) * np.repeat(np.exp2(scales.astype(np.float64) - 127.0), 8, axis=1)[..., None]
    return vals.transpose(0, 1, 3, 2).reshape(g * 512, n)


E2M1 = np.array([0.0, 0.5, 1.0, 1.5, 2.0, 3.0, 4.0, 6.0, -0.0, -0.5, -1.0, -1.5, -2.0, -3.0, -4.0, -6.0])


def pack_fp4(w):
    k, n = w.shape
    w = f64(np.asarray(w, np.float32).astype(ml_dtypes.bfloat16)).reshape(k // 32, 32, n)
    amax = np.abs(w).max(1)
    mant, ex = np.frexp(amax / 6.0)
    byte = np.clip(np.where(amax > 0, np.where(mant > 0.5, ex, ex - 1) + 127, 1), 1, 254)
    scaled = (w * np.exp2(127.0 - byte)[:, None, :]).reshape(k, n).astype(np.float32)
    c = np.ascontiguousarray(scaled.reshape(k // 512, 128, 4, n).transpose(0, 1, 3, 2)).astype(ml_dtypes.float4_e2m1fn).view(np.uint8) & 0xF
    words = (c[..., 0::2] | (c[..., 1::2] << 4)).reshape(k // 512, 128, 2 * n)
    return np.ascontiguousarray(words), np.ascontiguousarray(byte.astype(np.uint8).reshape(k // 512, 16, n))


def unpack_fp4(words, scales):
    g, _, n = scales.shape
    words = np.ascontiguousarray(words).reshape(g, 128, n, 2)
    nib = np.empty((g, 128, n, 4), np.uint8)
    nib[..., 0::2] = words & 0xF
    nib[..., 1::2] = words >> 4
    vals = E2M1[nib] * np.repeat(np.exp2(scales.astype(np.float64) - 127.0), 8, axis=1)[..., None]
    return vals.transpose(0, 1, 3, 2).reshape(g * 512, n)


def relu(v):
    return np.maximum(v, 0.0)


K, T, S, V, H, N = 512, 4096, 1024, 512, 512, 128


def setup_inputs():
    n = np.random.standard_normal
    s = mx_kscale(K)[:, None]
    u = mx_kscale(H)
    packed_xT = pack_weight(n((K, T)) * s)
    packed_w2 = pack_fp4(n((H, N)) / np.sqrt(2 * H) / u[:, None])
    packed_w3 = pack_fp4(n((H, N)) / np.sqrt(2 * H) / u[:, None])
    return {
        "x_words": packed_xT[0],
        "x_scales": packed_xT[1],
        "w1": (n((K, H)) / np.sqrt(K) / s * u).astype(np.float32),
        "w2_words": packed_w2[0],
        "w2_scales": packed_w2[1],
        "w3_words": packed_w3[0],
        "w3_scales": packed_w3[1],
        "offs": striped(np.random.permutation(T)[:S]),
    }


def reference(x_words, x_scales, w1, w2_words, w2_scales, w3_words, w3_scales, offs):
    xq = unpack_weight(x_words, x_scales)[:, unstriped(offs)]
    h = relu(mxq(f64(w1), 0, "e4m3").T @ xq)
    low = 0.5 * (h[:, :V] + h[:, V:2 * V])
    high = 0.5 * (h[:, :V] - h[:, V:2 * V])
    return unpack_fp4(w2_words, w2_scales).T @ mxq(low, 0, "e4m3") + unpack_fp4(w3_words, w3_scales).T @ mxq(high, 0, "e4m3")

@@ -1,0 +1,155 @@
+from contextlib import ExitStack
+
+import concourse.mybir as mybir
+
+K, T, S, V, H, N = 512, 4096, 1024, 512, 512, 128
+FLOPS = 2 * K * H * S + 2 * 2 * H * N * V
+
+F32 = mybir.dt.float32
+BF16 = mybir.dt.bfloat16
+I32 = mybir.dt.int32
+U32 = mybir.dt.uint32
+U16 = mybir.dt.uint16
+U8 = mybir.dt.uint8
+FP8X4 = mybir.dt.float8_e4m3fn_x4
+FP4X4 = mybir.dt.float4_e2m1fn_x4
+ALU = mybir.AluOpType
+ACT = mybir.ActivationFunctionType
+
+P = 128
+PACK = 4
+CH = 128
+NCH = V // CH
+
+
+def tile_picked_haar_relu_p_kernel(
+    tc, x_words, x_scales, w1, w2_words, w2_scales, w3_words, w3_scales, offs, out
+):
+    nc = tc.nc
+    with ExitStack() as ctx:
+        keep = ctx.enter_context(tc.tile_pool(name="keep", bufs=1))
+        psum = ctx.enter_context(tc.psum_pool(name="psum", bufs=4))
+
+        offsets = keep.tile([P, S // 16], U16, name="offsets")
+        nc.sync.dma_start(offsets[:], offs)
+
+        xs_all = keep.tile([P, T], U8, name="xs_all", align_bytes=64)
+        nc.vector.memset(xs_all[:].bitcast(I32), 0)
+        xs_rows = x_scales[0].rearrange("(q r) c -> r q c", r=4)
+        for r in range(4):
+            nc.scalar.dma_start(xs_all[r:P:32, :].bitcast(I32), xs_rows[r].bitcast(I32))
+
+        w1_raw = keep.tile([P, PACK, H], F32, name="w1_raw", align_bytes=64)
+        nc.sync.dma_start(w1_raw[:], w1.rearrange("(p j) c -> p j c", j=PACK))
+        xw_all = keep.tile([P, T], I32, name="xw_all", align_bytes=64)
+        nc.sync.dma_start(xw_all[:], x_words[0].rearrange("p c r -> p (c r)").bitcast(I32))
+
+        wb_words = keep.tile([P, 2, 2 * N], U8, name="wb_words", align_bytes=64)
+        wb_scales = keep.tile([P, 2, N], U8, name="wb_scales", align_bytes=64)
+        nc.vector.memset(wb_scales[:].rearrange("p b n -> p (b n)").bitcast(I32), 0)
+        for b, (words, scales) in enumerate(((w2_words, w2_scales), (w3_words, w3_scales))):
+            nc.sync.dma_start(wb_words[:, b, :].bitcast(I32), words[0].bitcast(I32))
+            rows = scales[0].rearrange("(q r) c -> r q c", r=4)
+            for r in range(4):
+                nc.sync.dma_start(wb_scales[r:P:32, b, :].bitcast(I32), rows[r].bitcast(I32))
+
+        xs = keep.tile([P, S], U8, name="xs", align_bytes=64)
+        nc.vector.tensor_copy(xs[:], xs_all[:].indirect(offsets[:]))
+
+        w1_bf = keep.tile([P, PACK * H], BF16, name="w1_bf", align_bytes=64)
+        nc.scalar.copy(
+            w1_bf[:].rearrange("p (t m j) -> p m t j", t=PACK, j=PACK),
+            w1_raw[:].rearrange("p j (m t) -> p m t j", t=PACK),
+        )
+        w1_codes = keep.tile([P, H], U32, name="w1_codes", align_bytes=64)
+        w1_scales = keep.tile([P, H], U8, name="w1_scales", align_bytes=64)
+        nc.vector.quantize_mx(out=w1_codes[:].bitcast(FP8X4), scales=w1_scales[:], in_=w1_bf[:])
+
+        early0 = V - CH
+        xw_early = keep.tile([P, S - early0], U32, name="xw_early", align_bytes=64)
+        nc.vector.tensor_copy(xw_early[:], xw_all[:].bitcast(U32).indirect(offsets[:, early0 // 16 :]))
+        xw_late = keep.tile([P, V], U32, name="xw_late", align_bytes=64)
+        nc.vector.tensor_copy(xw_late[:], xw_all[:].bitcast(U32).indirect(offsets[:, : V // 16]))
+
+        def picked_words(e0):
+            if e0 >= early0:
+                return xw_early[:, e0 - early0 : e0 - early0 + CH]
+            return xw_late[:, e0 : e0 + CH]
+
+        def first_product(d, c):
+            acc = psum.tile([P, PACK, CH], F32, name=f"h{d}_{c}", tag=f"piece{d}")
+            for t in range(PACK):
+                nc.tensor.matmul_mx(
+                    out=acc[:, t, :],
+                    lhsT=w1_codes[:, t * P : (t + 1) * P].bitcast(FP8X4),
+                    lhsT_scale=w1_scales[:, t * P : (t + 1) * P],
+                    rhs=picked_words(d * V + c * CH).bitcast(FP8X4),
+                    rhs_scale=xs[:, d * V + c * CH : d * V + (c + 1) * CH],
+                    start=True,
+                    stop=True,
+                )
+            return acc[:].rearrange("p t v -> p v t")
+
+        pre0, h1, bands = {}, {}, {}
+
+        def piece1(c):
+            pre = first_product(1, c)
+            h1[c] = keep.tile([P, CH, PACK], F32, name=f"h1_sb{c}", align_bytes=64)
+            nc.scalar.activation(h1[c][:], pre, ACT.Relu)
+
+        def piece0(c):
+            pre0[c] = first_product(0, c)
+
+        def band(c, b):
+            if b == 0:
+                bands[c] = keep.tile([P, 2, CH * PACK], BF16, name=f"bands{c}", align_bytes=64)
+            nc.vector.scalar_tensor_tensor(
+                bands[c][:, b, :].rearrange("p (v t) -> p v t", t=PACK),
+                pre0[c], 0.0, h1[c][:], ALU.max, (ALU.add, ALU.subtract)[b],
+            )
+
+        codes, bscales = {}, {}
+
+        def quantise(c, parts):
+            codes[c] = keep.tile([P, 2 * CH], U32, name=f"codes{c}", align_bytes=64)
+            bscales[c] = keep.tile([P, 2 * CH], U8, name=f"bscales{c}", align_bytes=64)
+            w = 2 * CH // parts
+            flat = bands[c][:].rearrange("p b x -> p (b x)")
+            for i in range(parts):
+                nc.vector.quantize_mx(
+                    out=codes[c][:, i * w : (i + 1) * w].bitcast(FP8X4),
+                    scales=bscales[c][:, i * w : (i + 1) * w],
+                    in_=flat[:, i * w * PACK : (i + 1) * w * PACK],
+                )
+
+        def second_product(c):
+            acc = psum.tile([N, CH], F32, name=f"o{c}", tag="piece1")
+            for b in range(2):
+                nc.tensor.matmul_mx(
+                    out=acc[:],
+                    lhsT=wb_words[:, b, :].bitcast(FP4X4),
+                    lhsT_scale=wb_scales[:, b, :],
+                    rhs=codes[c][:, b * CH : (b + 1) * CH].bitcast(FP8X4),
+                    rhs_scale=bscales[c][:, b * CH : (b + 1) * CH],
+                    start=(b == 0),
+                    stop=(b == 1),
+                )
+            res = keep.tile([N, CH], F32, name=f"res{c}")
+            nc.scalar.activation(res[:], acc[:], ACT.Copy, scale=0.5)
+            nc.sync.dma_start(out[:, c * CH : (c + 1) * CH], res[:])
+
+        order = [NCH - 1] + list(range(NCH - 1))
+        for c in order[:3]:
+            piece1(c)
+            piece0(c)
+        for i, c in enumerate(order):
+            band(c, 0)
+            if i > 0:
+                quantise(order[i - 1], 1)
+                second_product(order[i - 1])
+            band(c, 1)
+            if i == 1:
+                piece1(order[3])
+                piece0(order[3])
+        quantise(order[-1], 2)
+        second_product(order[-1])

@@ -33,20 +33,22 @@ def tile_picked_haar_relu_p_kernel(
         offsets = keep.tile([P, S // 16], U16, name="offsets")
         nc.sync.dma_start(offsets[:], offs)
 
-        xs_all = keep.tile([P, T], U8, name="xs_all", align_bytes=64)
+        xs_all = keep.tile([P, T], U8, name="xs_all", tag="scales", align_bytes=64)
         nc.vector.memset(xs_all[:].bitcast(I32), 0)
-        xs_rows = x_scales[0].rearrange("(q r) c -> r q c", r=4)
-        for r in range(4):
-            nc.scalar.dma_start(xs_all[r:P:32, :].bitcast(I32), xs_rows[r].bitcast(I32))
-
         w1_raw = keep.tile([P, PACK, H], F32, name="w1_raw", align_bytes=64)
         nc.sync.dma_start(w1_raw[:], w1.rearrange("(p j) c -> p j c", j=PACK))
-        xw_all = keep.tile([P, T], I32, name="xw_all", align_bytes=64)
+        xs_rows = x_scales[0].rearrange("(q r) c -> r q c", r=4)
+        for r in range(4):
+            nc.sync.dma_start(xs_all[r:P:32, :].bitcast(I32), xs_rows[r].bitcast(I32))
+
+        wb_scales = keep.tile([P, 2, N], U8, name="wb_scales", align_bytes=64)
+        zeros = keep.tile([P, 2 * N // 4], I32, name="zeros", tag="words", align_bytes=64)
+        nc.vector.memset(zeros[:], 0)
+        nc.vector.tensor_copy(wb_scales[:].rearrange("p b n -> p (b n)").bitcast(I32), zeros[:])
+        xw_all = keep.tile([P, T], I32, name="xw_all", tag="words", align_bytes=64)
         nc.sync.dma_start(xw_all[:], x_words[0].rearrange("p c r -> p (c r)").bitcast(I32))
 
         wb_words = keep.tile([P, 2, 2 * N], U8, name="wb_words", align_bytes=64)
-        wb_scales = keep.tile([P, 2, N], U8, name="wb_scales", align_bytes=64)
-        nc.vector.memset(wb_scales[:].rearrange("p b n -> p (b n)").bitcast(I32), 0)
         for b, (words, scales) in enumerate(((w2_words, w2_scales), (w3_words, w3_scales))):
             nc.sync.dma_start(wb_words[:, b, :].bitcast(I32), words[0].bitcast(I32))
             rows = scales[0].rearrange("(q r) c -> r q c", r=4)
@@ -62,7 +64,7 @@ def tile_picked_haar_relu_p_kernel(
             w1_raw[:].rearrange("p j (m t) -> p m t j", t=PACK),
         )
         w1_codes = keep.tile([P, H], U32, name="w1_codes", align_bytes=64)
-        w1_scales = keep.tile([P, H], U8, name="w1_scales", align_bytes=64)
+        w1_scales = keep.tile([P, H], U8, name="w1_scales", tag="scales", align_bytes=64)
         nc.vector.quantize_mx(out=w1_codes[:].bitcast(FP8X4), scales=w1_scales[:], in_=w1_bf[:])
 
         early0 = V - CH

@@ -30,33 +30,38 @@ def tile_picked_haar_relu_p_kernel(
         keep = ctx.enter_context(tc.tile_pool(name="keep", bufs=1))
         psum = ctx.enter_context(tc.psum_pool(name="psum", bufs=4))
 
+        reuse = ctx.enter_context(tc.tile_pool(name="reuse", bufs=1))
+
+        w1_raw = keep.tile([P, PACK, H], F32, name="w1_raw", align_bytes=64)
+        nc.sync.dma_start(w1_raw[:], w1.rearrange("(p j) c -> p j c", j=PACK))
         offsets = keep.tile([P, S // 16], U16, name="offsets")
         nc.sync.dma_start(offsets[:], offs)
 
-        xs_all = keep.tile([P, T], U8, name="xs_all", tag="scales", align_bytes=64)
+        xs_all = reuse.tile([P, T], U8, name="xs_all", offset=0, align_bytes=64)
         nc.vector.memset(xs_all[:].bitcast(I32), 0)
-        w1_raw = keep.tile([P, PACK, H], F32, name="w1_raw", align_bytes=64)
-        nc.sync.dma_start(w1_raw[:], w1.rearrange("(p j) c -> p j c", j=PACK))
-        xs_rows = x_scales[0].rearrange("(q r) c -> r q c", r=4)
-        for r in range(4):
-            nc.sync.dma_start(xs_all[r:P:32, :].bitcast(I32), xs_rows[r].bitcast(I32))
+        nc.sync.dma_start(xs_all[0:P:8, :].bitcast(I32), x_scales[0].bitcast(I32))
 
-        wb_scales = keep.tile([P, 2, N], U8, name="wb_scales", align_bytes=64)
-        zeros = keep.tile([P, 2 * N // 4], I32, name="zeros", tag="words", align_bytes=64)
+        xs = keep.tile([P, S], U8, name="xs", align_bytes=64)
+        zeros = keep.tile([P, S // 4], I32, name="zeros", tag="words", align_bytes=64)
         nc.vector.memset(zeros[:], 0)
-        nc.vector.tensor_copy(wb_scales[:].rearrange("p b n -> p (b n)").bitcast(I32), zeros[:])
+        nc.vector.tensor_copy(xs[:].bitcast(I32), zeros[:])
         xw_all = keep.tile([P, T], I32, name="xw_all", tag="words", align_bytes=64)
         nc.sync.dma_start(xw_all[:], x_words[0].rearrange("p c r -> p (c r)").bitcast(I32))
 
-        wb_words = keep.tile([P, 2, 2 * N], U8, name="wb_words", align_bytes=64)
-        for b, (words, scales) in enumerate(((w2_words, w2_scales), (w3_words, w3_scales))):
+        xs_spread = keep.tile([P, S], U8, name="xs_spread", align_bytes=64)
+        nc.vector.tensor_copy(xs_spread[:], xs_all[:].indirect(offsets[:]))
+        for r in range(4):
+            nc.sync.dma_start(xs[r:P:32, :].bitcast(I32), xs_spread[8 * r : P : 32, :].bitcast(I32))
+
+        wb_words = reuse.tile([P, 2, 2 * N], U8, name="wb_words", offset=512, align_bytes=64)
+        wb_scales = reuse.tile([P, 2, N], U8, name="wb_scales", offset=1024, align_bytes=64)
+        nc.vector.memset(wb_scales[:].rearrange("p b n -> p (b n)").bitcast(I32), 0)
+        for b, words in enumerate((w2_words, w3_words)):
             nc.sync.dma_start(wb_words[:, b, :].bitcast(I32), words[0].bitcast(I32))
+        for b, scales in enumerate((w2_scales, w3_scales)):
             rows = scales[0].rearrange("(q r) c -> r q c", r=4)
             for r in range(4):
                 nc.sync.dma_start(wb_scales[r:P:32, b, :].bitcast(I32), rows[r].bitcast(I32))
-
-        xs = keep.tile([P, S], U8, name="xs", align_bytes=64)
-        nc.vector.tensor_copy(xs[:], xs_all[:].indirect(offsets[:]))
 
         w1_bf = keep.tile([P, PACK * H], BF16, name="w1_bf", align_bytes=64)
         nc.scalar.copy(
@@ -64,19 +69,27 @@ def tile_picked_haar_relu_p_kernel(
             w1_raw[:].rearrange("p j (m t) -> p m t j", t=PACK),
         )
         w1_codes = keep.tile([P, H], U32, name="w1_codes", align_bytes=64)
-        w1_scales = keep.tile([P, H], U8, name="w1_scales", tag="scales", align_bytes=64)
+        w1_scales = reuse.tile([P, H], U8, name="w1_scales", offset=0, align_bytes=64)
         nc.vector.quantize_mx(out=w1_codes[:].bitcast(FP8X4), scales=w1_scales[:], in_=w1_bf[:])
 
-        early0 = V - CH
-        xw_early = keep.tile([P, S - early0], U32, name="xw_early", align_bytes=64)
-        nc.vector.tensor_copy(xw_early[:], xw_all[:].bitcast(U32).indirect(offsets[:, early0 // 16 :]))
-        xw_late = keep.tile([P, V], U32, name="xw_late", align_bytes=64)
-        nc.vector.tensor_copy(xw_late[:], xw_all[:].bitcast(U32).indirect(offsets[:, : V // 16]))
+        warm = psum.tile([P, H], F32, name="warm", tag="piece0")
+        for i in range(2):
+            nc.tensor.matmul_mx(
+                out=warm[:],
+                lhsT=w1_codes[:, :P].bitcast(FP8X4),
+                lhsT_scale=w1_scales[:, :P],
+                rhs=w1_codes[:].bitcast(FP8X4),
+                rhs_scale=w1_scales[:],
+                start=True,
+                stop=True,
+            )
 
-        def picked_words(e0):
-            if e0 >= early0:
-                return xw_early[:, e0 - early0 : e0 - early0 + CH]
-            return xw_late[:, e0 : e0 + CH]
+        xw = {}
+        for d in (1, 0):
+            xw[d] = keep.tile([P, V], U32, name=f"xw{d}", align_bytes=64)
+            nc.vector.tensor_copy(
+                xw[d][:], xw_all[:].bitcast(U32).indirect(offsets[:, d * V // 16 : (d + 1) * V // 16])
+            )
 
         def first_product(d, c):
             acc = psum.tile([P, PACK, CH], F32, name=f"h{d}_{c}", tag=f"piece{d}")
@@ -85,7 +98,7 @@ def tile_picked_haar_relu_p_kernel(
                     out=acc[:, t, :],
                     lhsT=w1_codes[:, t * P : (t + 1) * P].bitcast(FP8X4),
                     lhsT_scale=w1_scales[:, t * P : (t + 1) * P],
-                    rhs=picked_words(d * V + c * CH).bitcast(FP8X4),
+                    rhs=xw[d][:, c * CH : (c + 1) * CH].bitcast(FP8X4),
                     rhs_scale=xs[:, d * V + c * CH : d * V + (c + 1) * CH],
                     start=True,
                     stop=True,
@@ -103,17 +116,31 @@ def tile_picked_haar_relu_p_kernel(
             pre0[c] = first_product(0, c)
 
         def band(c, b):
-            if b == 0:
+            if c not in bands:
                 bands[c] = keep.tile([P, 2, CH * PACK], BF16, name=f"bands{c}", align_bytes=64)
             nc.vector.scalar_tensor_tensor(
                 bands[c][:, b, :].rearrange("p (v t) -> p v t", t=PACK),
                 pre0[c], 0.0, h1[c][:], ALU.max, (ALU.add, ALU.subtract)[b],
             )
 
+        def bands_on_gpsimd(c):
+            h0 = reuse.tile([P, CH, PACK], F32, name="h0_sb", offset=2048, align_bytes=64)
+            nc.scalar.activation(h0[:], pre0[c], ACT.Relu)
+            bands[c] = keep.tile([P, 2, CH * PACK], BF16, name=f"bands{c}", align_bytes=64)
+            nc.gpsimd.tensor_tensor(
+                bands[c][:, 1, :],
+                h0[:].rearrange("p v t -> p (v t)"),
+                h1[c][:].rearrange("p v t -> p (v t)"),
+                ALU.subtract,
+            )
+
         codes, bscales = {}, {}
 
         def quantise(c, parts):
-            codes[c] = keep.tile([P, 2 * CH], U32, name=f"codes{c}", align_bytes=64)
+            if c in (0, 2):
+                codes[c] = reuse.tile([P, 2 * CH], U32, name=f"codes{c}", offset=2048 + 512 * c, align_bytes=64)
+            else:
+                codes[c] = keep.tile([P, 2 * CH], U32, name=f"codes{c}", align_bytes=64)
             bscales[c] = keep.tile([P, 2 * CH], U8, name=f"bscales{c}", align_bytes=64)
             w = 2 * CH // parts
             flat = bands[c][:].rearrange("p b x -> p (b x)")
@@ -140,18 +167,24 @@ def tile_picked_haar_relu_p_kernel(
             nc.scalar.activation(res[:], acc[:], ACT.Copy, scale=0.5)
             nc.sync.dma_start(out[:, c * CH : (c + 1) * CH], res[:])
 
-        order = [NCH - 1] + list(range(NCH - 1))
-        for c in order[:3]:
+        for c in range(3):
             piece1(c)
+        for c in range(3):
             piece0(c)
-        for i, c in enumerate(order):
+        bands_on_gpsimd(1)
+        piece1(3)
+        piece0(3)
+        for c in (0, 2):
             band(c, 0)
-            if i > 0:
-                quantise(order[i - 1], 1)
-                second_product(order[i - 1])
             band(c, 1)
-            if i == 1:
-                piece1(order[3])
-                piece0(order[3])
-        quantise(order[-1], 2)
-        second_product(order[-1])
+        band(1, 0)
+        quantise(0, 1)
+        second_product(0)
+        band(3, 0)
+        quantise(2, 1)
+        second_product(2)
+        quantise(1, 1)
+        second_product(1)
+        band(3, 1)
+        quantise(3, 2)
+        second_product(3)

@@ -20,6 +20,7 @@ P = 128
 PACK = 4
 CH = 128
 NCH = V // CH
+GP = 32
 
 
 def tile_picked_haar_relu_p_kernel(
@@ -30,6 +31,7 @@ def tile_picked_haar_relu_p_kernel(
         keep = ctx.enter_context(tc.tile_pool(name="keep", bufs=1))
         psum = ctx.enter_context(tc.psum_pool(name="psum", bufs=4))
 
+        ring = ctx.enter_context(tc.tile_pool(name="ring", bufs=7))
         reuse = ctx.enter_context(tc.tile_pool(name="reuse", bufs=1))
 
         w1_raw = keep.tile([P, PACK, H], F32, name="w1_raw", align_bytes=64)
@@ -84,12 +86,16 @@ def tile_picked_haar_relu_p_kernel(
                 stop=True,
             )
 
-        xw = {}
-        for d in (1, 0):
-            xw[d] = keep.tile([P, V], U32, name=f"xw{d}", align_bytes=64)
-            nc.vector.tensor_copy(
-                xw[d][:], xw_all[:].bitcast(U32).indirect(offsets[:, d * V // 16 : (d + 1) * V // 16])
-            )
+        early0 = V - CH
+        xw_early = keep.tile([P, S - early0], U32, name="xw_early", align_bytes=64)
+        nc.vector.tensor_copy(xw_early[:], xw_all[:].bitcast(U32).indirect(offsets[:, early0 // 16 :]))
+        xw_late = keep.tile([P, V], U32, name="xw_late", align_bytes=64)
+        nc.vector.tensor_copy(xw_late[:], xw_all[:].bitcast(U32).indirect(offsets[:, : V // 16]))
+
+        def picked_words(e0):
+            if e0 >= early0:
+                return xw_early[:, e0 - early0 : e0 - early0 + CH]
+            return xw_late[:, e0 : e0 + CH]
 
         def first_product(d, c):
             acc = psum.tile([P, PACK, CH], F32, name=f"h{d}_{c}", tag=f"piece{d}")
@@ -98,7 +104,7 @@ def tile_picked_haar_relu_p_kernel(
                     out=acc[:, t, :],
                     lhsT=w1_codes[:, t * P : (t + 1) * P].bitcast(FP8X4),
                     lhsT_scale=w1_scales[:, t * P : (t + 1) * P],
-                    rhs=xw[d][:, c * CH : (c + 1) * CH].bitcast(FP8X4),
+                    rhs=picked_words(d * V + c * CH).bitcast(FP8X4),
                     rhs_scale=xs[:, d * V + c * CH : d * V + (c + 1) * CH],
                     start=True,
                     stop=True,
@@ -115,51 +121,57 @@ def tile_picked_haar_relu_p_kernel(
         def piece0(c):
             pre0[c] = first_product(0, c)
 
+        def band_tile(c, b):
+            bands[c, b] = ring.tile([P, CH, PACK], BF16, name=f"band{c}_{b}", tag="band", align_bytes=64)
+            return bands[c, b][:]
+
         def band(c, b):
-            if c not in bands:
-                bands[c] = keep.tile([P, 2, CH * PACK], BF16, name=f"bands{c}", align_bytes=64)
             nc.vector.scalar_tensor_tensor(
-                bands[c][:, b, :].rearrange("p (v t) -> p v t", t=PACK),
-                pre0[c], 0.0, h1[c][:], ALU.max, (ALU.add, ALU.subtract)[b],
+                band_tile(c, b), pre0[c], 0.0, h1[c][:], ALU.max, (ALU.add, ALU.subtract)[b]
             )
 
-        def bands_on_gpsimd(c):
+        def shared_bands(c):
             h0 = reuse.tile([P, CH, PACK], F32, name="h0_sb", offset=2048, align_bytes=64)
             nc.scalar.activation(h0[:], pre0[c], ACT.Relu)
-            bands[c] = keep.tile([P, 2, CH * PACK], BF16, name=f"bands{c}", align_bytes=64)
-            nc.gpsimd.tensor_tensor(
-                bands[c][:, 1, :],
-                h0[:].rearrange("p v t -> p (v t)"),
-                h1[c][:].rearrange("p v t -> p (v t)"),
-                ALU.subtract,
+            nc.gpsimd.tensor_tensor(band_tile(c, 1), h0[:], h1[c][:], ALU.subtract)
+            low = band_tile(c, 0)
+            nc.gpsimd.tensor_tensor(low[:, :GP, :], h0[:, :GP, :], h1[c][:, :GP, :], ALU.add)
+            nc.vector.scalar_tensor_tensor(
+                low[:, GP:, :], pre0[c][:, GP:, :], 0.0, h1[c][:, GP:, :], ALU.max, ALU.add
             )
 
-        codes, bscales = {}, {}
+        piece1(3)
+        piece0(3)
+        piece1(0)
+        piece0(0)
+        band(3, 0)
+        band(3, 1)
+        shared_bands(0)
+        for c in (1, 2):
+            piece1(c)
+            piece0(c)
 
-        def quantise(c, parts):
-            if c in (0, 2):
-                codes[c] = reuse.tile([P, 2 * CH], U32, name=f"codes{c}", offset=2048 + 512 * c, align_bytes=64)
-            else:
-                codes[c] = keep.tile([P, 2 * CH], U32, name=f"codes{c}", align_bytes=64)
-            bscales[c] = keep.tile([P, 2 * CH], U8, name=f"bscales{c}", align_bytes=64)
-            w = 2 * CH // parts
-            flat = bands[c][:].rearrange("p b x -> p (b x)")
-            for i in range(parts):
-                nc.vector.quantize_mx(
-                    out=codes[c][:, i * w : (i + 1) * w].bitcast(FP8X4),
-                    scales=bscales[c][:, i * w : (i + 1) * w],
-                    in_=flat[:, i * w * PACK : (i + 1) * w * PACK],
-                )
+        codes = reuse.tile([P, NCH, 2, CH], U32, name="codes", offset=2048, align_bytes=64)
+        bscales = keep.tile([P, NCH, 2, CH], U8, name="bscales", align_bytes=64)
 
-        def second_product(c):
+        def quantise(c, b):
+            nc.vector.quantize_mx(
+                out=codes[:, c, b, :].bitcast(FP8X4),
+                scales=bscales[:, c, b, :],
+                in_=bands[c, b][:].rearrange("p v t -> p (v t)"),
+            )
+
+        def finish(c):
+            for b in range(2):
+                quantise(c, b)
             acc = psum.tile([N, CH], F32, name=f"o{c}", tag="piece1")
             for b in range(2):
                 nc.tensor.matmul_mx(
                     out=acc[:],
                     lhsT=wb_words[:, b, :].bitcast(FP4X4),
                     lhsT_scale=wb_scales[:, b, :],
-                    rhs=codes[c][:, b * CH : (b + 1) * CH].bitcast(FP8X4),
-                    rhs_scale=bscales[c][:, b * CH : (b + 1) * CH],
+                    rhs=codes[:, c, b, :].bitcast(FP8X4),
+                    rhs_scale=bscales[:, c, b, :],
                     start=(b == 0),
                     stop=(b == 1),
                 )
@@ -167,24 +179,10 @@ def tile_picked_haar_relu_p_kernel(
             nc.scalar.activation(res[:], acc[:], ACT.Copy, scale=0.5)
             nc.sync.dma_start(out[:, c * CH : (c + 1) * CH], res[:])
 
-        for c in range(3):
-            piece1(c)
-        for c in range(3):
-            piece0(c)
-        bands_on_gpsimd(1)
-        piece1(3)
-        piece0(3)
-        for c in (0, 2):
-            band(c, 0)
-            band(c, 1)
         band(1, 0)
-        quantise(0, 1)
-        second_product(0)
-        band(3, 0)
-        quantise(2, 1)
-        second_product(2)
-        quantise(1, 1)
-        second_product(1)
-        band(3, 1)
-        quantise(3, 2)
-        second_product(3)
+        band(1, 1)
+        band(2, 0)
+        for c in (3, 1, 0):
+            finish(c)
+        band(2, 1)
+        finish(2)

@@ -21,6 +21,7 @@ PACK = 4
 CH = 128
 NCH = V // CH
 GP = 32
+CUT = T - 640
 
 
 def tile_picked_haar_relu_p_kernel(
@@ -44,22 +45,26 @@ def tile_picked_haar_relu_p_kernel(
         nc.sync.dma_start(xs_all[0:P:8, :].bitcast(I32), x_scales[0].bitcast(I32))
 
         xs = keep.tile([P, S], U8, name="xs", align_bytes=64)
-        zeros = keep.tile([P, S // 4], I32, name="zeros", tag="words", align_bytes=64)
+        zeros = reuse.tile([P, S // 4], I32, name="zeros", offset=24576 - 512, align_bytes=64)
         nc.vector.memset(zeros[:], 0)
         nc.vector.tensor_copy(xs[:].bitcast(I32), zeros[:])
-        xw_all = keep.tile([P, T], I32, name="xw_all", tag="words", align_bytes=64)
-        nc.sync.dma_start(xw_all[:], x_words[0].rearrange("p c r -> p (c r)").bitcast(I32))
+        xw_all = reuse.tile([P, T], I32, name="xw_all", offset=8192, align_bytes=64)
+        words_in = x_words[0].rearrange("p c r -> p (c r)").bitcast(I32)
+        nc.sync.dma_start(xw_all[:, :CUT], words_in[:, :CUT])
+        w2_sb = reuse.tile([P, 2 * N], U8, name="w2_sb", offset=24576, align_bytes=64)
+        nc.sync.dma_start(w2_sb[:].bitcast(I32), w2_words[0].bitcast(I32))
+        nc.sync.dma_start(xw_all[:, CUT:], words_in[:, CUT:])
 
         xs_spread = keep.tile([P, S], U8, name="xs_spread", align_bytes=64)
         nc.vector.tensor_copy(xs_spread[:], xs_all[:].indirect(offsets[:]))
         for r in range(4):
             nc.sync.dma_start(xs[r:P:32, :].bitcast(I32), xs_spread[8 * r : P : 32, :].bitcast(I32))
 
-        wb_words = reuse.tile([P, 2, 2 * N], U8, name="wb_words", offset=512, align_bytes=64)
+        w3_sb = reuse.tile([P, 2 * N], U8, name="w3_sb", offset=512, align_bytes=64)
+        wb_words = (w2_sb, w3_sb)
         wb_scales = reuse.tile([P, 2, N], U8, name="wb_scales", offset=1024, align_bytes=64)
         nc.vector.memset(wb_scales[:].rearrange("p b n -> p (b n)").bitcast(I32), 0)
-        for b, words in enumerate((w2_words, w3_words)):
-            nc.sync.dma_start(wb_words[:, b, :].bitcast(I32), words[0].bitcast(I32))
+        nc.sync.dma_start(w3_sb[:].bitcast(I32), w3_words[0].bitcast(I32))
         for b, scales in enumerate((w2_scales, w3_scales)):
             rows = scales[0].rearrange("(q r) c -> r q c", r=4)
             for r in range(4):
@@ -75,13 +80,13 @@ def tile_picked_haar_relu_p_kernel(
         nc.vector.quantize_mx(out=w1_codes[:].bitcast(FP8X4), scales=w1_scales[:], in_=w1_bf[:])
 
         warm = psum.tile([P, H], F32, name="warm", tag="piece0")
-        for i in range(2):
+        for n in (H, H, H // 2):
             nc.tensor.matmul_mx(
-                out=warm[:],
-                lhsT=w1_codes[:, :P].bitcast(FP8X4),
+                out=warm[:, :n],
+                lhsT=w2_sb[:].bitcast(FP4X4),
                 lhsT_scale=w1_scales[:, :P],
-                rhs=w1_codes[:].bitcast(FP8X4),
-                rhs_scale=w1_scales[:],
+                rhs=w1_codes[:, :n].bitcast(FP8X4),
+                rhs_scale=w1_scales[:, :n],
                 start=True,
                 stop=True,
             )
@@ -168,7 +173,7 @@ def tile_picked_haar_relu_p_kernel(
             for b in range(2):
                 nc.tensor.matmul_mx(
                     out=acc[:],
-                    lhsT=wb_words[:, b, :].bitcast(FP4X4),
+                    lhsT=wb_words[b][:].bitcast(FP4X4),
                     lhsT_scale=wb_scales[:, b, :],
                     rhs=codes[:, c, b, :].bitcast(FP8X4),
                     rhs_scale=bscales[:, c, b, :],

@@ -21,7 +21,7 @@ PACK = 4
 CH = 128
 NCH = V // CH
 GP = 32
-CUT = T - 640
+CUT = T // 2
 
 
 def tile_picked_haar_relu_p_kernel(
@@ -32,7 +32,6 @@ def tile_picked_haar_relu_p_kernel(
         keep = ctx.enter_context(tc.tile_pool(name="keep", bufs=1))
         psum = ctx.enter_context(tc.psum_pool(name="psum", bufs=4))
 
-        ring = ctx.enter_context(tc.tile_pool(name="ring", bufs=7))
         reuse = ctx.enter_context(tc.tile_pool(name="reuse", bufs=1))
 
         w1_raw = keep.tile([P, PACK, H], F32, name="w1_raw", align_bytes=64)
@@ -42,7 +41,7 @@ def tile_picked_haar_relu_p_kernel(
 
         xs_all = reuse.tile([P, T], U8, name="xs_all", offset=0, align_bytes=64)
         nc.vector.memset(xs_all[:].bitcast(I32), 0)
-        nc.sync.dma_start(xs_all[0:P:8, :].bitcast(I32), x_scales[0].bitcast(I32))
+        nc.sync.dma_start(xs_all[32:96:4, :].bitcast(I32), x_scales[0].bitcast(I32))
 
         xs = keep.tile([P, S], U8, name="xs", align_bytes=64)
         zeros = reuse.tile([P, S // 4], I32, name="zeros", offset=24576 - 512, align_bytes=64)
@@ -50,20 +49,20 @@ def tile_picked_haar_relu_p_kernel(
         nc.vector.tensor_copy(xs[:].bitcast(I32), zeros[:])
         xw_all = reuse.tile([P, T], I32, name="xw_all", offset=8192, align_bytes=64)
         words_in = x_words[0].rearrange("p c r -> p (c r)").bitcast(I32)
+        nc.scalar.dma_start(xw_all[:, CUT:], words_in[:, CUT:])
         nc.sync.dma_start(xw_all[:, :CUT], words_in[:, :CUT])
-        w2_sb = reuse.tile([P, 2 * N], U8, name="w2_sb", offset=24576, align_bytes=64)
-        nc.sync.dma_start(w2_sb[:].bitcast(I32), w2_words[0].bitcast(I32))
-        nc.sync.dma_start(xw_all[:, CUT:], words_in[:, CUT:])
+        w2_sb = reuse.tile([P, 2 * N], U8, name="w2_sb", offset=1536, align_bytes=64)
 
         xs_spread = keep.tile([P, S], U8, name="xs_spread", align_bytes=64)
         nc.vector.tensor_copy(xs_spread[:], xs_all[:].indirect(offsets[:]))
         for r in range(4):
-            nc.sync.dma_start(xs[r:P:32, :].bitcast(I32), xs_spread[8 * r : P : 32, :].bitcast(I32))
+            nc.sync.dma_start(xs[r:P:32, :].bitcast(I32), xs_spread[32 + 4 * r : 96 : 16, :].bitcast(I32))
 
         w3_sb = reuse.tile([P, 2 * N], U8, name="w3_sb", offset=512, align_bytes=64)
         wb_words = (w2_sb, w3_sb)
         wb_scales = reuse.tile([P, 2, N], U8, name="wb_scales", offset=1024, align_bytes=64)
         nc.vector.memset(wb_scales[:].rearrange("p b n -> p (b n)").bitcast(I32), 0)
+        nc.sync.dma_start(w2_sb[:].bitcast(I32), w2_words[0].bitcast(I32))
         nc.sync.dma_start(w3_sb[:].bitcast(I32), w3_words[0].bitcast(I32))
         for b, scales in enumerate((w2_scales, w3_scales)):
             rows = scales[0].rearrange("(q r) c -> r q c", r=4)
@@ -83,7 +82,7 @@ def tile_picked_haar_relu_p_kernel(
         for n in (H, H, H // 2):
             nc.tensor.matmul_mx(
                 out=warm[:, :n],
-                lhsT=w2_sb[:].bitcast(FP4X4),
+                lhsT=w1_codes[:, :P].bitcast(FP8X4),
                 lhsT_scale=w1_scales[:, :P],
                 rhs=w1_codes[:, :n].bitcast(FP8X4),
                 rhs_scale=w1_scales[:, :n],
@@ -127,8 +126,12 @@ def tile_picked_haar_relu_p_kernel(
             pre0[c] = first_product(0, c)
 
         def band_tile(c, b):
-            bands[c, b] = ring.tile([P, CH, PACK], BF16, name=f"band{c}_{b}", tag="band", align_bytes=64)
-            return bands[c, b][:]
+            if c == 2:
+                bands[c, b] = reuse.tile([P, CH, PACK], BF16, name=f"band2_{b}", offset=(34816, 28672)[b], align_bytes=64)
+                return bands[c, b][:]
+            if c not in bands:
+                bands[c] = reuse.tile([P, 2, CH, PACK], BF16, name=f"bands{c}", offset={3: 28672, 1: 30720, 0: 32768}[c], align_bytes=64)
+            return bands[c][:, b]
 
         def band(c, b):
             nc.vector.scalar_tensor_tensor(
@@ -167,8 +170,15 @@ def tile_picked_haar_relu_p_kernel(
             )
 
         def finish(c):
-            for b in range(2):
-                quantise(c, b)
+            if c == 2:
+                for b in range(2):
+                    quantise(c, b)
+            else:
+                nc.vector.quantize_mx(
+                    out=codes[:, c].rearrange("p b v -> p (b v)").bitcast(FP8X4),
+                    scales=bscales[:, c].rearrange("p b v -> p (b v)"),
+                    in_=bands[c][:].rearrange("p b v t -> p (b v t)"),
+                )
             acc = psum.tile([N, CH], F32, name=f"o{c}", tag="piece1")
             for b in range(2):
                 nc.tensor.matmul_mx(

@@ -21,6 +21,7 @@ PACK = 4
 CH = 128
 NCH = V // CH
 GP = 32
+SM = 88
 CUT = T // 2
 
 
@@ -70,10 +71,10 @@ def tile_picked_haar_relu_p_kernel(
                 nc.sync.dma_start(wb_scales[r:P:32, b, :].bitcast(I32), rows[r].bitcast(I32))
 
         w1_bf = keep.tile([P, PACK * H], BF16, name="w1_bf", align_bytes=64)
-        nc.scalar.copy(
-            w1_bf[:].rearrange("p (t m j) -> p m t j", t=PACK, j=PACK),
-            w1_raw[:].rearrange("p j (m t) -> p m t j", t=PACK),
-        )
+        cast_out = w1_bf[:].rearrange("p (t m j) -> p m t j", t=PACK, j=PACK)
+        cast_in = w1_raw[:].rearrange("p j (m t) -> p m t j", t=PACK)
+        nc.scalar.copy(cast_out[:, :SM], cast_in[:, :SM])
+        nc.vector.tensor_copy(cast_out[:, SM:], cast_in[:, SM:])
         w1_codes = keep.tile([P, H], U32, name="w1_codes", align_bytes=64)
         w1_scales = reuse.tile([P, H], U8, name="w1_scales", offset=0, align_bytes=64)
         nc.vector.quantize_mx(out=w1_codes[:].bitcast(FP8X4), scales=w1_scales[:], in_=w1_bf[:])

@@ -20,7 +20,7 @@ P = 128
 PACK = 4
 CH = 128
 NCH = V // CH
-GP = 32
+GP = 104
 SM = 88
 CUT = T // 2
 
@@ -31,7 +31,7 @@ def tile_picked_haar_relu_p_kernel(
     nc = tc.nc
     with ExitStack() as ctx:
         keep = ctx.enter_context(tc.tile_pool(name="keep", bufs=1))
-        psum = ctx.enter_context(tc.psum_pool(name="psum", bufs=4))
+        psum = ctx.enter_context(tc.psum_pool(name="psum", bufs=1))
 
         reuse = ctx.enter_context(tc.tile_pool(name="reuse", bufs=1))
 
@@ -79,7 +79,7 @@ def tile_picked_haar_relu_p_kernel(
         w1_scales = reuse.tile([P, H], U8, name="w1_scales", offset=0, align_bytes=64)
         nc.vector.quantize_mx(out=w1_codes[:].bitcast(FP8X4), scales=w1_scales[:], in_=w1_bf[:])
 
-        warm = psum.tile([P, H], F32, name="warm", tag="piece0")
+        warm = psum.tile([P, H], F32, name="warm", tag="bank6")
         for n in (H, H, H // 2):
             nc.tensor.matmul_mx(
                 out=warm[:, :n],
@@ -102,8 +102,11 @@ def tile_picked_haar_relu_p_kernel(
                 return xw_early[:, e0 - early0 : e0 - early0 + CH]
             return xw_late[:, e0 : e0 + CH]
 
+        first_bank = {(1, 3): 0, (0, 3): 1, (1, 0): 2, (1, 2): 3, (0, 0): 4, (0, 2): 5, (1, 1): 1, (0, 1): 3}
+        out_bank = {3: 0, 0: 2, 2: 7, 1: 6}
+
         def first_product(d, c):
-            acc = psum.tile([P, PACK, CH], F32, name=f"h{d}_{c}", tag=f"piece{d}")
+            acc = psum.tile([P, PACK, CH], F32, name=f"h{d}_{c}", tag=f"bank{first_bank[d, c]}")
             for t in range(PACK):
                 nc.tensor.matmul_mx(
                     out=acc[:, t, :],
@@ -127,38 +130,39 @@ def tile_picked_haar_relu_p_kernel(
             pre0[c] = first_product(0, c)
 
         def band_tile(c, b):
-            if c == 2:
-                bands[c, b] = reuse.tile([P, CH, PACK], BF16, name=f"band2_{b}", offset=(34816, 28672)[b], align_bytes=64)
+            if c == 1:
+                if (c, b) not in bands:
+                    bands[c, b] = reuse.tile([P, CH, PACK], BF16, name=f"band1_{b}", offset=(34816, 28672)[b], align_bytes=64)
                 return bands[c, b][:]
             if c not in bands:
-                bands[c] = reuse.tile([P, 2, CH, PACK], BF16, name=f"bands{c}", offset={3: 28672, 1: 30720, 0: 32768}[c], align_bytes=64)
+                bands[c] = reuse.tile([P, 2, CH, PACK], BF16, name=f"bands{c}", offset={3: 28672, 0: 30720, 2: 32768}[c], align_bytes=64)
             return bands[c][:, b]
 
-        def band(c, b):
+        def band(c, b, v0=0):
             nc.vector.scalar_tensor_tensor(
-                band_tile(c, b), pre0[c], 0.0, h1[c][:], ALU.max, (ALU.add, ALU.subtract)[b]
-            )
-
-        def shared_bands(c):
-            h0 = reuse.tile([P, CH, PACK], F32, name="h0_sb", offset=2048, align_bytes=64)
-            nc.scalar.activation(h0[:], pre0[c], ACT.Relu)
-            nc.gpsimd.tensor_tensor(band_tile(c, 1), h0[:], h1[c][:], ALU.subtract)
-            low = band_tile(c, 0)
-            nc.gpsimd.tensor_tensor(low[:, :GP, :], h0[:, :GP, :], h1[c][:, :GP, :], ALU.add)
-            nc.vector.scalar_tensor_tensor(
-                low[:, GP:, :], pre0[c][:, GP:, :], 0.0, h1[c][:, GP:, :], ALU.max, ALU.add
+                band_tile(c, b)[:, v0:, :], pre0[c][:, v0:, :], 0.0, h1[c][:, v0:, :], ALU.max, (ALU.add, ALU.subtract)[b]
             )
 
         piece1(3)
         piece0(3)
-        piece1(0)
-        piece0(0)
+        h0_early = keep.tile([P, CH, PACK], F32, name="h0_early", align_bytes=64)
+        nc.vector.tensor_scalar_max(h0_early[:], pre0[3], 0.0)
+        nc.gpsimd.tensor_tensor(band_tile(3, 1), h0_early[:], h1[3][:], ALU.subtract)
         band(3, 0)
-        band(3, 1)
-        shared_bands(0)
-        for c in (1, 2):
-            piece1(c)
-            piece0(c)
+        piece1(0)
+        piece1(2)
+        piece0(0)
+        piece0(2)
+        h0_late = reuse.tile([P, GP, PACK], F32, name="h0_late", offset=2048, align_bytes=64)
+        nc.scalar.activation(h0_late[:], pre0[2][:, :GP, :], ACT.Relu)
+        nc.gpsimd.tensor_tensor(band_tile(2, 1)[:, :GP, :], h0_late[:], h1[2][:, :GP, :], ALU.subtract)
+        piece1(1)
+        band(0, 0)
+        band(0, 1)
+        piece0(1)
+        band(2, 0)
+        band(2, 1, GP)
+        band(1, 0)
 
         codes = reuse.tile([P, NCH, 2, CH], U32, name="codes", offset=2048, align_bytes=64)
         bscales = keep.tile([P, NCH, 2, CH], U8, name="bscales", align_bytes=64)
@@ -171,7 +175,7 @@ def tile_picked_haar_relu_p_kernel(
             )
 
         def finish(c):
-            if c == 2:
+            if c == 1:
                 for b in range(2):
                     quantise(c, b)
             else:
@@ -180,7 +184,7 @@ def tile_picked_haar_relu_p_kernel(
                     scales=bscales[:, c].rearrange("p b v -> p (b v)"),
                     in_=bands[c][:].rearrange("p b v t -> p (b v t)"),
                 )
-            acc = psum.tile([N, CH], F32, name=f"o{c}", tag="piece1")
+            acc = psum.tile([N, CH], F32, name=f"o{c}", tag=f"bank{out_bank[c]}")
             for b in range(2):
                 nc.tensor.matmul_mx(
                     out=acc[:],
@@ -195,10 +199,7 @@ def tile_picked_haar_relu_p_kernel(
             nc.scalar.activation(res[:], acc[:], ACT.Copy, scale=0.5)
             nc.sync.dma_start(out[:, c * CH : (c + 1) * CH], res[:])
 
-        band(1, 0)
-        band(1, 1)
-        band(2, 0)
-        for c in (3, 1, 0):
+        for c in (3, 0, 2):
             finish(c)
-        band(2, 1)
-        finish(2)
+        band(1, 1)
+        finish(1)

@@ -65,7 +65,7 @@ def tile_picked_haar_relu_p_kernel(
         nc.vector.memset(wb_scales[:].rearrange("p b n -> p (b n)").bitcast(I32), 0)
         nc.sync.dma_start(w2_sb[:].bitcast(I32), w2_words[0].bitcast(I32))
         nc.sync.dma_start(w3_sb[:].bitcast(I32), w3_words[0].bitcast(I32))
-        for b, scales in enumerate((w2_scales, w3_scales)):
+        for b, scales in ((1, w3_scales), (0, w2_scales)):
             rows = scales[0].rearrange("(q r) c -> r q c", r=4)
             for r in range(4):
                 nc.sync.dma_start(wb_scales[r:P:32, b, :].bitcast(I32), rows[r].bitcast(I32))
@@ -164,13 +164,13 @@ def tile_picked_haar_relu_p_kernel(
         band(2, 1, GP)
         band(1, 0)
 
-        codes = reuse.tile([P, NCH, 2, CH], U32, name="codes", offset=2048, align_bytes=64)
-        bscales = keep.tile([P, NCH, 2, CH], U8, name="bscales", align_bytes=64)
+        codes = [reuse.tile([P, 2 * CH], U32, name=f"codes{c}", offset=2048 + 1024 * ((c + 1) % NCH), align_bytes=64) for c in range(NCH)]
+        bscales = [keep.tile([P, 2 * CH], U8, name=f"bscales{c}", align_bytes=64) for c in range(NCH)]
 
         def quantise(c, b):
             nc.vector.quantize_mx(
-                out=codes[:, c, b, :].bitcast(FP8X4),
-                scales=bscales[:, c, b, :],
+                out=codes[c][:, b * CH : (b + 1) * CH].bitcast(FP8X4),
+                scales=bscales[c][:, b * CH : (b + 1) * CH],
                 in_=bands[c, b][:].rearrange("p v t -> p (v t)"),
             )
 
@@ -180,8 +180,8 @@ def tile_picked_haar_relu_p_kernel(
                     quantise(c, b)
             else:
                 nc.vector.quantize_mx(
-                    out=codes[:, c].rearrange("p b v -> p (b v)").bitcast(FP8X4),
-                    scales=bscales[:, c].rearrange("p b v -> p (b v)"),
+                    out=codes[c][:].bitcast(FP8X4),
+                    scales=bscales[c][:],
                     in_=bands[c][:].rearrange("p b v t -> p (b v t)"),
                 )
             acc = psum.tile([N, CH], F32, name=f"o{c}", tag=f"bank{out_bank[c]}")
@@ -190,8 +190,8 @@ def tile_picked_haar_relu_p_kernel(
                     out=acc[:],
                     lhsT=wb_words[b][:].bitcast(FP4X4),
                     lhsT_scale=wb_scales[:, b, :],
-                    rhs=codes[:, c, b, :].bitcast(FP8X4),
-                    rhs_scale=bscales[:, c, b, :],
+                    rhs=codes[c][:, b * CH : (b + 1) * CH].bitcast(FP8X4),
+                    rhs_scale=bscales[c][:, b * CH : (b + 1) * CH],
                     start=(b == 0),
                     stop=(b == 1),
                 )

@@ -20,7 +20,7 @@ P = 128
 PACK = 4
 CH = 128
 NCH = V // CH
-GP = 104
+GP = 128
 SM = 88
 CUT = T // 2
 
@@ -132,7 +132,7 @@ def tile_picked_haar_relu_p_kernel(
         def band_tile(c, b):
             if c == 1:
                 if (c, b) not in bands:
-                    bands[c, b] = reuse.tile([P, CH, PACK], BF16, name=f"band1_{b}", offset=(34816, 28672)[b], align_bytes=64)
+                    bands[c, b] = reuse.tile([P, CH, PACK], BF16, name=f"band1_{b}", offset=(34816, 35840)[b], align_bytes=64)
                 return bands[c, b][:]
             if c not in bands:
                 bands[c] = reuse.tile([P, 2, CH, PACK], BF16, name=f"bands{c}", offset={3: 28672, 0: 30720, 2: 32768}[c], align_bytes=64)
@@ -161,8 +161,8 @@ def tile_picked_haar_relu_p_kernel(
         band(0, 1)
         piece0(1)
         band(2, 0)
-        band(2, 1, GP)
         band(1, 0)
+        band(1, 1)
 
         codes = [reuse.tile([P, 2 * CH], U32, name=f"codes{c}", offset=2048 + 1024 * ((c + 1) % NCH), align_bytes=64) for c in range(NCH)]
         bscales = [keep.tile([P, 2 * CH], U8, name=f"bscales{c}", align_bytes=64) for c in range(NCH)]
@@ -201,5 +201,4 @@ def tile_picked_haar_relu_p_kernel(
 
         for c in (3, 0, 2):
             finish(c)
-        band(1, 1)
         finish(1)

@@ -77,12 +77,15 @@ def tile_picked_haar_relu_p_kernel(
         nc.vector.tensor_copy(cast_out[:, SM:], cast_in[:, SM:])
         w1_codes = keep.tile([P, H], U32, name="w1_codes", align_bytes=64)
         w1_scales = reuse.tile([P, H], U8, name="w1_scales", offset=0, align_bytes=64)
-        nc.vector.quantize_mx(out=w1_codes[:].bitcast(FP8X4), scales=w1_scales[:], in_=w1_bf[:])
+        nc.vector.quantize_mx(out=w1_codes[:, :P].bitcast(FP8X4), scales=w1_scales[:, :P], in_=w1_bf[:, : PACK * P])
+        nc.vector.quantize_mx(out=w1_codes[:, P : 2 * P].bitcast(FP8X4), scales=w1_scales[:, P : 2 * P], in_=w1_bf[:, PACK * P : 2 * PACK * P])
+        nc.vector.quantize_mx(out=w1_codes[:, 2 * P :].bitcast(FP8X4), scales=w1_scales[:, 2 * P :], in_=w1_bf[:, 2 * PACK * P :])
 
         warm = psum.tile([P, H], F32, name="warm", tag="bank6")
-        for n in (H, H, H // 2):
+        for i in range(10):
+            n = P
             nc.tensor.matmul_mx(
-                out=warm[:, :n],
+                out=warm[:, i % PACK * P : (i % PACK + 1) * P],
                 lhsT=w1_codes[:, :P].bitcast(FP8X4),
                 lhsT_scale=w1_scales[:, :P],
                 rhs=w1_codes[:, :n].bitcast(FP8X4),

@@ -21,7 +21,7 @@ PACK = 4
 CH = 128
 NCH = V // CH
 GP = 128
-SM = 88
+SM = 64
 CUT = T // 2
 
 

@@ -22,6 +22,8 @@ CH = 128
 NCH = V // CH
 GP = 128
 SM = 64
+WARM_M = 32
+WARM_PASSES = 17
 CUT = T // 2
 
 
@@ -82,12 +84,12 @@ def tile_picked_haar_relu_p_kernel(
         nc.vector.quantize_mx(out=w1_codes[:, 2 * P :].bitcast(FP8X4), scales=w1_scales[:, 2 * P :], in_=w1_bf[:, 2 * PACK * P :])
 
         warm = psum.tile([P, H], F32, name="warm", tag="bank6")
-        for i in range(10):
+        for i in range(WARM_PASSES):
             n = P
             nc.tensor.matmul_mx(
-                out=warm[:, i % PACK * P : (i % PACK + 1) * P],
-                lhsT=w1_codes[:, :P].bitcast(FP8X4),
-                lhsT_scale=w1_scales[:, :P],
+                out=warm[:WARM_M, i % PACK * P : (i % PACK + 1) * P],
+                lhsT=w1_codes[:, :WARM_M].bitcast(FP8X4),
+                lhsT_scale=w1_scales[:, :WARM_M],
                 rhs=w1_codes[:, :n].bitcast(FP8X4),
                 rhs_scale=w1_scales[:, :n],
                 start=True,

@@ -23,7 +23,7 @@ NCH = V // CH
 GP = 128
 SM = 64
 WARM_M = 32
-WARM_PASSES = 17
+WARM_PASSES = 4
 CUT = T // 2
 
 
@@ -79,19 +79,16 @@ def tile_picked_haar_relu_p_kernel(
         nc.vector.tensor_copy(cast_out[:, SM:], cast_in[:, SM:])
         w1_codes = keep.tile([P, H], U32, name="w1_codes", align_bytes=64)
         w1_scales = reuse.tile([P, H], U8, name="w1_scales", offset=0, align_bytes=64)
-        nc.vector.quantize_mx(out=w1_codes[:, :P].bitcast(FP8X4), scales=w1_scales[:, :P], in_=w1_bf[:, : PACK * P])
-        nc.vector.quantize_mx(out=w1_codes[:, P : 2 * P].bitcast(FP8X4), scales=w1_scales[:, P : 2 * P], in_=w1_bf[:, PACK * P : 2 * PACK * P])
-        nc.vector.quantize_mx(out=w1_codes[:, 2 * P :].bitcast(FP8X4), scales=w1_scales[:, 2 * P :], in_=w1_bf[:, 2 * PACK * P :])
+        nc.vector.quantize_mx(out=w1_codes[:].bitcast(FP8X4), scales=w1_scales[:], in_=w1_bf[:])
 
-        warm = psum.tile([P, H], F32, name="warm", tag="bank6")
         for i in range(WARM_PASSES):
-            n = P
+            warm = psum.tile([P, H], F32, name=f"warm{i}", tag=f"bank{4 + i}")
             nc.tensor.matmul_mx(
-                out=warm[:WARM_M, i % PACK * P : (i % PACK + 1) * P],
+                out=warm[:WARM_M, :],
                 lhsT=w1_codes[:, :WARM_M].bitcast(FP8X4),
                 lhsT_scale=w1_scales[:, :WARM_M],
-                rhs=w1_codes[:, :n].bitcast(FP8X4),
-                rhs_scale=w1_scales[:, :n],
+                rhs=w1_codes[:].bitcast(FP8X4),
+                rhs_scale=w1_scales[:],
                 start=True,
                 stop=True,
             )

@@ -21,9 +21,9 @@ PACK = 4
 CH = 128
 NCH = V // CH
 GP = 128
-SM = 64
+SM = 48
 WARM_M = 32
-WARM_PASSES = 4
+WARM_PASSES = 3
 CUT = T // 2
 
 
@@ -63,14 +63,8 @@ def tile_picked_haar_relu_p_kernel(
 
         w3_sb = reuse.tile([P, 2 * N], U8, name="w3_sb", offset=512, align_bytes=64)
         wb_words = (w2_sb, w3_sb)
-        wb_scales = reuse.tile([P, 2, N], U8, name="wb_scales", offset=1024, align_bytes=64)
-        nc.vector.memset(wb_scales[:].rearrange("p b n -> p (b n)").bitcast(I32), 0)
         nc.sync.dma_start(w2_sb[:].bitcast(I32), w2_words[0].bitcast(I32))
         nc.sync.dma_start(w3_sb[:].bitcast(I32), w3_words[0].bitcast(I32))
-        for b, scales in ((1, w3_scales), (0, w2_scales)):
-            rows = scales[0].rearrange("(q r) c -> r q c", r=4)
-            for r in range(4):
-                nc.sync.dma_start(wb_scales[r:P:32, b, :].bitcast(I32), rows[r].bitcast(I32))
 
         w1_bf = keep.tile([P, PACK * H], BF16, name="w1_bf", align_bytes=64)
         cast_out = w1_bf[:].rearrange("p (t m j) -> p m t j", t=PACK, j=PACK)
@@ -80,6 +74,13 @@ def tile_picked_haar_relu_p_kernel(
         w1_codes = keep.tile([P, H], U32, name="w1_codes", align_bytes=64)
         w1_scales = reuse.tile([P, H], U8, name="w1_scales", offset=0, align_bytes=64)
         nc.vector.quantize_mx(out=w1_codes[:].bitcast(FP8X4), scales=w1_scales[:], in_=w1_bf[:])
+
+        wb_scales = reuse.tile([P, 2, N], U8, name="wb_scales", offset=1024, align_bytes=64)
+        nc.vector.memset(wb_scales[:].rearrange("p b n -> p (b n)").bitcast(I32), 0)
+        for b, scales in ((1, w3_scales), (0, w2_scales)):
+            rows = scales[0].rearrange("(q r) c -> r q c", r=4)
+            for r in range(4):
+                nc.sync.dma_start(wb_scales[r:P:32, b, :].bitcast(I32), rows[r].bitcast(I32))
 
         for i in range(WARM_PASSES):
             warm = psum.tile([P, H], F32, name=f"warm{i}", tag=f"bank{4 + i}")

@@ -1,6 +1,7 @@
 from contextlib import ExitStack
 
 import concourse.mybir as mybir
+from concourse.masks import make_identity
 
 K, T, S, V, H, N = 512, 4096, 1024, 512, 512, 128
 FLOPS = 2 * K * H * S + 2 * 2 * H * N * V
@@ -20,10 +21,9 @@ P = 128
 PACK = 4
 CH = 128
 NCH = V // CH
-GP = 128
 SM = 48
-WARM_M = 32
-WARM_PASSES = 3
+WARM_WIDTHS = (512, 512, 256)
+GP = 80
 CUT = T // 2
 
 
@@ -82,126 +82,112 @@ def tile_picked_haar_relu_p_kernel(
             for r in range(4):
                 nc.sync.dma_start(wb_scales[r:P:32, b, :].bitcast(I32), rows[r].bitcast(I32))
 
-        for i in range(WARM_PASSES):
-            warm = psum.tile([P, H], F32, name=f"warm{i}", tag=f"bank{4 + i}")
+        for i, width in enumerate(WARM_WIDTHS):
+            warm = psum.tile([P, H], F32, name=f"warm{i}", tag=f"bank{5 + i}")
             nc.tensor.matmul_mx(
-                out=warm[:WARM_M, :],
-                lhsT=w1_codes[:, :WARM_M].bitcast(FP8X4),
-                lhsT_scale=w1_scales[:, :WARM_M],
+                out=warm[:, :width],
+                lhsT=w1_codes[:, :P].bitcast(FP8X4),
+                lhsT_scale=w1_scales[:, :P],
+                rhs=w1_codes[:, :width].bitcast(FP8X4),
+                rhs_scale=w1_scales[:, :width],
+                start=True,
+                stop=True,
+            )
+
+        xw = [keep.tile([P, V], U32, name=f"xw{d}", align_bytes=64) for d in range(2)]
+        for d in (1, 0):
+            nc.vector.tensor_copy(xw[d][:], xw_all[:].bitcast(U32).indirect(offsets[:, d * V // 16 : (d + 1) * V // 16]))
+
+        identity = keep.tile([P, P], F32, name="identity", align_bytes=64)
+        make_identity(nc, identity[:])
+
+        def turned_product(d, c, bank):
+            acc = psum.tile([CH, H], F32, name=f"ht{d}_{c}", tag=f"bank{bank}")
+            nc.tensor.matmul_mx(
+                out=acc[:],
+                lhsT=xw[d][:, c * CH : (c + 1) * CH].bitcast(FP8X4),
+                lhsT_scale=xs[:, d * V + c * CH : d * V + (c + 1) * CH],
                 rhs=w1_codes[:].bitcast(FP8X4),
                 rhs_scale=w1_scales[:],
                 start=True,
                 stop=True,
             )
+            return acc
 
-        early0 = V - CH
-        xw_early = keep.tile([P, S - early0], U32, name="xw_early", align_bytes=64)
-        nc.vector.tensor_copy(xw_early[:], xw_all[:].bitcast(U32).indirect(offsets[:, early0 // 16 :]))
-        xw_late = keep.tile([P, V], U32, name="xw_late", align_bytes=64)
-        nc.vector.tensor_copy(xw_late[:], xw_all[:].bitcast(U32).indirect(offsets[:, : V // 16]))
-
-        def picked_words(e0):
-            if e0 >= early0:
-                return xw_early[:, e0 - early0 : e0 - early0 + CH]
-            return xw_late[:, e0 : e0 + CH]
-
-        first_bank = {(1, 3): 0, (0, 3): 1, (1, 0): 2, (1, 2): 3, (0, 0): 4, (0, 2): 5, (1, 1): 1, (0, 1): 3}
-        out_bank = {3: 0, 0: 2, 2: 7, 1: 6}
-
-        def first_product(d, c):
-            acc = psum.tile([P, PACK, CH], F32, name=f"h{d}_{c}", tag=f"bank{first_bank[d, c]}")
+        def first_product(d, c, bank):
+            acc = psum.tile([P, PACK, CH], F32, name=f"h{d}_{c}", tag=f"bank{bank}")
             for t in range(PACK):
                 nc.tensor.matmul_mx(
                     out=acc[:, t, :],
                     lhsT=w1_codes[:, t * P : (t + 1) * P].bitcast(FP8X4),
                     lhsT_scale=w1_scales[:, t * P : (t + 1) * P],
-                    rhs=picked_words(d * V + c * CH).bitcast(FP8X4),
+                    rhs=xw[d][:, c * CH : (c + 1) * CH].bitcast(FP8X4),
                     rhs_scale=xs[:, d * V + c * CH : d * V + (c + 1) * CH],
                     start=True,
                     stop=True,
                 )
             return acc[:].rearrange("p t v -> p v t")
 
-        pre0, h1, bands = {}, {}, {}
+        bands = [keep.tile([P, 2, CH, PACK], BF16, name=f"bands{c}", align_bytes=64) for c in range(NCH)]
+        h0_sb = reuse.tile([P, GP, PACK], F32, name="h0_sb", offset=2048, align_bytes=64)
+        h1 = {c: keep.tile([P, CH, PACK], F32, name=f"h1_{c}", align_bytes=64) for c in (0, 1, 3)}
 
-        def piece1(c):
-            pre = first_product(1, c)
-            h1[c] = keep.tile([P, CH, PACK], F32, name=f"h1_sb{c}", align_bytes=64)
-            nc.scalar.activation(h1[c][:], pre, ACT.Relu)
+        def both_bands(c, v0):
+            for b, op in enumerate((ALU.add, ALU.subtract)):
+                nc.vector.scalar_tensor_tensor(bands[c][:, b, v0:], pre0[c][:, v0:], 0.0, h1[c][:, v0:], ALU.max, op)
 
-        def piece0(c):
-            pre0[c] = first_product(0, c)
+        pre_t1 = turned_product(1, 2, 0)
+        pre1 = {0: first_product(1, 0, 1), 3: first_product(1, 3, 2), 1: first_product(1, 1, 6)}
+        pre0 = {0: first_product(0, 0, 3), 3: first_product(0, 3, 5)}
+        pre_t0 = turned_product(0, 2, 4)
+        pre0[1] = first_product(0, 1, 7)
 
-        def band_tile(c, b):
-            if c == 1:
-                if (c, b) not in bands:
-                    bands[c, b] = reuse.tile([P, CH, PACK], BF16, name=f"band1_{b}", offset=(34816, 35840)[b], align_bytes=64)
-                return bands[c, b][:]
-            if c not in bands:
-                bands[c] = reuse.tile([P, 2, CH, PACK], BF16, name=f"bands{c}", offset={3: 28672, 0: 30720, 2: 32768}[c], align_bytes=64)
-            return bands[c][:, b]
+        ht = [keep.tile([CH, H], F32, name=f"ht_sb{i}", align_bytes=64) for i in range(3)]
+        nc.scalar.activation(ht[1][:], pre_t1[:], ACT.Relu)
+        nc.gpsimd.tensor_scalar(ht[2][:], ht[1][:], -1.0, 0.0, ALU.mult, ALU.add)
+        nc.vector.tensor_scalar_max(h1[0][:], pre1[0], 0.0)
+        nc.scalar.activation(h1[3][:], pre1[3], ACT.Relu)
+        both_bands(0, 0)
+        nc.scalar.activation(h1[1][:], pre1[1], ACT.Relu)
+        nc.scalar.activation(h0_sb[:], pre0[3][:, :GP], ACT.Relu)
+        for b, op in enumerate((ALU.add, ALU.subtract)):
+            nc.gpsimd.tensor_tensor(bands[3][:, b, :GP], h0_sb[:], h1[3][:, :GP], op)
+        nc.scalar.activation(ht[0][:], pre_t0[:], ACT.Relu)
+        both_bands(1, 0)
+        both_bands(3, GP)
+        turned = [psum.tile([P, PACK, CH], F32, name=f"turned{b}", tag=f"bank{b}") for b in range(2)]
+        for b in range(2):
+            for t in range(PACK):
+                nc.tensor.matmul(turned[b][:, t, :], ht[1 + b][:, t * P : (t + 1) * P], identity[:], start=(t == 0), stop=False, is_transpose=True)
+        for b in range(2):
+            for t in range(PACK):
+                nc.tensor.matmul(turned[b][:, t, :], ht[0][:, t * P : (t + 1) * P], identity[:], start=False, stop=(t == PACK - 1), is_transpose=True)
+            nc.scalar.copy(bands[2][:, b], turned[b][:].rearrange("p t v -> p v t"))
 
-        def band(c, b, v0=0):
-            nc.vector.scalar_tensor_tensor(
-                band_tile(c, b)[:, v0:, :], pre0[c][:, v0:, :], 0.0, h1[c][:, v0:, :], ALU.max, (ALU.add, ALU.subtract)[b]
-            )
-
-        piece1(3)
-        piece0(3)
-        h0_early = keep.tile([P, CH, PACK], F32, name="h0_early", align_bytes=64)
-        nc.vector.tensor_scalar_max(h0_early[:], pre0[3], 0.0)
-        nc.gpsimd.tensor_tensor(band_tile(3, 1), h0_early[:], h1[3][:], ALU.subtract)
-        band(3, 0)
-        piece1(0)
-        piece1(2)
-        piece0(0)
-        piece0(2)
-        h0_late = reuse.tile([P, GP, PACK], F32, name="h0_late", offset=2048, align_bytes=64)
-        nc.scalar.activation(h0_late[:], pre0[2][:, :GP, :], ACT.Relu)
-        nc.gpsimd.tensor_tensor(band_tile(2, 1)[:, :GP, :], h0_late[:], h1[2][:, :GP, :], ALU.subtract)
-        piece1(1)
-        band(0, 0)
-        band(0, 1)
-        piece0(1)
-        band(2, 0)
-        band(1, 0)
-        band(1, 1)
-
-        codes = [reuse.tile([P, 2 * CH], U32, name=f"codes{c}", offset=2048 + 1024 * ((c + 1) % NCH), align_bytes=64) for c in range(NCH)]
-        bscales = [keep.tile([P, 2 * CH], U8, name=f"bscales{c}", align_bytes=64) for c in range(NCH)]
-
-        def quantise(c, b):
-            nc.vector.quantize_mx(
-                out=codes[c][:, b * CH : (b + 1) * CH].bitcast(FP8X4),
-                scales=bscales[c][:, b * CH : (b + 1) * CH],
-                in_=bands[c, b][:].rearrange("p v t -> p (v t)"),
-            )
-
-        def finish(c):
-            if c == 1:
-                for b in range(2):
-                    quantise(c, b)
-            else:
+        codes = {0: reuse.tile([P, 2 * CH], U32, name="codes0", offset=2048, align_bytes=64)}
+        for c in (1, 2, 3):
+            codes[c] = keep.tile([P, 2 * CH], U32, name=f"codes{c}", align_bytes=64)
+        for c in (0, 1, 3, 2):
+            bscales = keep.tile([P, 2 * CH], U8, name=f"bscales{c}", align_bytes=64)
+            widths = (CH, CH) if c == 2 else (2 * CH,)
+            flat = bands[c][:].rearrange("p b v t -> p (b v t)")
+            for i, w in enumerate(widths):
                 nc.vector.quantize_mx(
-                    out=codes[c][:].bitcast(FP8X4),
-                    scales=bscales[c][:],
-                    in_=bands[c][:].rearrange("p b v t -> p (b v t)"),
+                    out=codes[c][:, i * w : (i + 1) * w].bitcast(FP8X4),
+                    scales=bscales[:, i * w : (i + 1) * w],
+                    in_=flat[:, i * w * PACK : (i + 1) * w * PACK],
                 )
-            acc = psum.tile([N, CH], F32, name=f"o{c}", tag=f"bank{out_bank[c]}")
+            acc = psum.tile([N, CH], F32, name=f"o{c}", tag=f"bank{(2, 4, 6, 3)[c]}")
             for b in range(2):
                 nc.tensor.matmul_mx(
                     out=acc[:],
                     lhsT=wb_words[b][:].bitcast(FP4X4),
                     lhsT_scale=wb_scales[:, b, :],
                     rhs=codes[c][:, b * CH : (b + 1) * CH].bitcast(FP8X4),
-                    rhs_scale=bscales[c][:, b * CH : (b + 1) * CH],
+                    rhs_scale=bscales[:, b * CH : (b + 1) * CH],
                     start=(b == 0),
                     stop=(b == 1),
                 )
             res = keep.tile([N, CH], F32, name=f"res{c}")
             nc.scalar.activation(res[:], acc[:], ACT.Copy, scale=0.5)
             nc.sync.dma_start(out[:, c * CH : (c + 1) * CH], res[:])
-
-        for c in (3, 0, 2):
-            finish(c)
-        finish(1)

@@ -23,7 +23,7 @@ CH = 128
 NCH = V // CH
 SM = 48
 WARM_WIDTHS = (512, 512, 256)
-GP = 80
+GP = 72
 CUT = T // 2
 
 
@@ -136,25 +136,27 @@ def tile_picked_haar_relu_p_kernel(
             for b, op in enumerate((ALU.add, ALU.subtract)):
                 nc.vector.scalar_tensor_tensor(bands[c][:, b, v0:], pre0[c][:, v0:], 0.0, h1[c][:, v0:], ALU.max, op)
 
-        pre_t1 = turned_product(1, 2, 0)
-        pre1 = {0: first_product(1, 0, 1), 3: first_product(1, 3, 2), 1: first_product(1, 1, 6)}
-        pre0 = {0: first_product(0, 0, 3), 3: first_product(0, 3, 5)}
-        pre_t0 = turned_product(0, 2, 4)
+        pre1 = {0: first_product(1, 0, 0)}
+        pre_t1 = turned_product(1, 2, 1)
+        pre1[3] = first_product(1, 3, 2)
+        pre0 = {0: first_product(0, 0, 3), 3: first_product(0, 3, 4)}
+        pre1[1] = first_product(1, 1, 5)
+        pre_t0 = turned_product(0, 2, 6)
         pre0[1] = first_product(0, 1, 7)
 
         ht = [keep.tile([CH, H], F32, name=f"ht_sb{i}", align_bytes=64) for i in range(3)]
-        nc.scalar.activation(ht[1][:], pre_t1[:], ACT.Relu)
+        nc.scalar.activation(h1[0][:], pre1[0], ACT.Relu)
+        nc.vector.tensor_scalar_max(ht[1][:], pre_t1[:], 0.0)
         nc.gpsimd.tensor_scalar(ht[2][:], ht[1][:], -1.0, 0.0, ALU.mult, ALU.add)
-        nc.vector.tensor_scalar_max(h1[0][:], pre1[0], 0.0)
         nc.scalar.activation(h1[3][:], pre1[3], ACT.Relu)
         both_bands(0, 0)
-        nc.scalar.activation(h1[1][:], pre1[1], ACT.Relu)
         nc.scalar.activation(h0_sb[:], pre0[3][:, :GP], ACT.Relu)
         for b, op in enumerate((ALU.add, ALU.subtract)):
             nc.gpsimd.tensor_tensor(bands[3][:, b, :GP], h0_sb[:], h1[3][:, :GP], op)
-        nc.scalar.activation(ht[0][:], pre_t0[:], ACT.Relu)
-        both_bands(1, 0)
         both_bands(3, GP)
+        nc.scalar.activation(h1[1][:], pre1[1], ACT.Relu)
+        both_bands(1, 0)
+        nc.scalar.activation(ht[0][:], pre_t0[:], ACT.Relu)
         turned = [psum.tile([P, PACK, CH], F32, name=f"turned{b}", tag=f"bank{b}") for b in range(2)]
         for b in range(2):
             for t in range(PACK):
@@ -169,7 +171,7 @@ def tile_picked_haar_relu_p_kernel(
             codes[c] = keep.tile([P, 2 * CH], U32, name=f"codes{c}", align_bytes=64)
         for c in (0, 1, 3, 2):
             bscales = keep.tile([P, 2 * CH], U8, name=f"bscales{c}", align_bytes=64)
-            widths = (CH, CH) if c == 2 else (2 * CH,)
+            widths = (CH, CH) if c in (0, 2) else (2 * CH,)
             flat = bands[c][:].rearrange("p b v t -> p (b v t)")
             for i, w in enumerate(widths):
                 nc.vector.quantize_mx(
@@ -177,7 +179,7 @@ def tile_picked_haar_relu_p_kernel(
                     scales=bscales[:, i * w : (i + 1) * w],
                     in_=flat[:, i * w * PACK : (i + 1) * w * PACK],
                 )
-            acc = psum.tile([N, CH], F32, name=f"o{c}", tag=f"bank{(2, 4, 6, 3)[c]}")
+            acc = psum.tile([N, CH], F32, name=f"o{c}", tag=f"bank{(2, 3, 6, 5)[c]}")
             for b in range(2):
                 nc.tensor.matmul_mx(
                     out=acc[:],

@@ -21,7 +21,7 @@ P = 128
 PACK = 4
 CH = 128
 NCH = V // CH
-SM = 48
+SM = 72
 WARM_WIDTHS = (512, 512, 256)
 GP = 72
 CUT = T // 2
@@ -69,7 +69,8 @@ def tile_picked_haar_relu_p_kernel(
         w1_bf = keep.tile([P, PACK * H], BF16, name="w1_bf", align_bytes=64)
         cast_out = w1_bf[:].rearrange("p (t m j) -> p m t j", t=PACK, j=PACK)
         cast_in = w1_raw[:].rearrange("p j (m t) -> p m t j", t=PACK)
-        nc.scalar.copy(cast_out[:, :SM], cast_in[:, :SM])
+        for t0 in (0, 2):
+            nc.scalar.copy(cast_out[:, :SM, t0 : t0 + 2], cast_in[:, :SM, t0 : t0 + 2])
         nc.vector.tensor_copy(cast_out[:, SM:], cast_in[:, SM:])
         w1_codes = keep.tile([P, H], U32, name="w1_codes", align_bytes=64)
         w1_scales = reuse.tile([P, H], U8, name="w1_scales", offset=0, align_bytes=64)
@@ -156,14 +157,18 @@ def tile_picked_haar_relu_p_kernel(
         both_bands(3, GP)
         nc.scalar.activation(h1[1][:], pre1[1], ACT.Relu)
         both_bands(1, 0)
-        nc.scalar.activation(ht[0][:], pre_t0[:], ACT.Relu)
+        for half in range(2):
+            cols = slice(half * H // 2, (half + 1) * H // 2)
+            nc.scalar.activation(ht[0][:, cols], pre_t0[:, cols], ACT.Relu)
         turned = [psum.tile([P, PACK, CH], F32, name=f"turned{b}", tag=f"bank{b}") for b in range(2)]
         for b in range(2):
             for t in range(PACK):
                 nc.tensor.matmul(turned[b][:, t, :], ht[1 + b][:, t * P : (t + 1) * P], identity[:], start=(t == 0), stop=False, is_transpose=True)
+        for t0 in (0, 2):
+            for b in range(2):
+                for t in (t0, t0 + 1):
+                    nc.tensor.matmul(turned[b][:, t, :], ht[0][:, t * P : (t + 1) * P], identity[:], start=False, stop=(t == PACK - 1), is_transpose=True)
         for b in range(2):
-            for t in range(PACK):
-                nc.tensor.matmul(turned[b][:, t, :], ht[0][:, t * P : (t + 1) * P], identity[:], start=False, stop=(t == PACK - 1), is_transpose=True)
             nc.scalar.copy(bands[2][:, b], turned[b][:].rearrange("p t v -> p v t"))
 
         codes = {0: reuse.tile([P, 2 * CH], U32, name="codes0", offset=2048, align_bytes=64)}
@@ -171,13 +176,11 @@ def tile_picked_haar_relu_p_kernel(
             codes[c] = keep.tile([P, 2 * CH], U32, name=f"codes{c}", align_bytes=64)
         for c in (0, 1, 3, 2):
             bscales = keep.tile([P, 2 * CH], U8, name=f"bscales{c}", align_bytes=64)
-            widths = (CH, CH) if c in (0, 2) else (2 * CH,)
-            flat = bands[c][:].rearrange("p b v t -> p (b v t)")
-            for i, w in enumerate(widths):
+            for b in range(2):
                 nc.vector.quantize_mx(
-                    out=codes[c][:, i * w : (i + 1) * w].bitcast(FP8X4),
-                    scales=bscales[:, i * w : (i + 1) * w],
-                    in_=flat[:, i * w * PACK : (i + 1) * w * PACK],
+                    out=codes[c][:, b * CH : (b + 1) * CH].bitcast(FP8X4),
+                    scales=bscales[:, b * CH : (b + 1) * CH],
+                    in_=bands[c][:, b].rearrange("p v t -> p (v t)"),
                 )
             acc = psum.tile([N, CH], F32, name=f"o{c}", tag=f"bank{(2, 3, 6, 5)[c]}")
             for b in range(2):

@@ -21,7 +21,7 @@ P = 128
 PACK = 4
 CH = 128
 NCH = V // CH
-SM = 72
+SM = 48
 WARM_WIDTHS = (512, 512, 256)
 GP = 72
 CUT = T // 2
@@ -69,8 +69,7 @@ def tile_picked_haar_relu_p_kernel(
         w1_bf = keep.tile([P, PACK * H], BF16, name="w1_bf", align_bytes=64)
         cast_out = w1_bf[:].rearrange("p (t m j) -> p m t j", t=PACK, j=PACK)
         cast_in = w1_raw[:].rearrange("p j (m t) -> p m t j", t=PACK)
-        for t0 in (0, 2):
-            nc.scalar.copy(cast_out[:, :SM, t0 : t0 + 2], cast_in[:, :SM, t0 : t0 + 2])
+        nc.scalar.copy(cast_out[:, :SM], cast_in[:, :SM])
         nc.vector.tensor_copy(cast_out[:, SM:], cast_in[:, SM:])
         w1_codes = keep.tile([P, H], U32, name="w1_codes", align_bytes=64)
         w1_scales = reuse.tile([P, H], U8, name="w1_scales", offset=0, align_bytes=64)

@@ -21,8 +21,8 @@ P = 128
 PACK = 4
 CH = 128
 NCH = V // CH
-SM = 48
-WARM_WIDTHS = (512, 512, 256)
+SM = 56
+WARM_WIDTHS = (256, 512, 512)
 GP = 72
 CUT = T // 2
 
@@ -70,10 +70,13 @@ def tile_picked_haar_relu_p_kernel(
         cast_out = w1_bf[:].rearrange("p (t m j) -> p m t j", t=PACK, j=PACK)
         cast_in = w1_raw[:].rearrange("p j (m t) -> p m t j", t=PACK)
         nc.scalar.copy(cast_out[:, :SM], cast_in[:, :SM])
-        nc.vector.tensor_copy(cast_out[:, SM:], cast_in[:, SM:])
+        for t0 in (0, 2):
+            nc.vector.tensor_copy(cast_out[:, SM:, t0 : t0 + 2], cast_in[:, SM:, t0 : t0 + 2])
         w1_codes = keep.tile([P, H], U32, name="w1_codes", align_bytes=64)
         w1_scales = reuse.tile([P, H], U8, name="w1_scales", offset=0, align_bytes=64)
-        nc.vector.quantize_mx(out=w1_codes[:].bitcast(FP8X4), scales=w1_scales[:], in_=w1_bf[:])
+        for t0 in (0, 2):
+            cols = slice(t0 * P, (t0 + 2) * P)
+            nc.vector.quantize_mx(out=w1_codes[:, cols].bitcast(FP8X4), scales=w1_scales[:, cols], in_=w1_bf[:, t0 * H : (t0 + 2) * H])
 
         wb_scales = reuse.tile([P, 2, N], U8, name="wb_scales", offset=1024, align_bytes=64)
         nc.vector.memset(wb_scales[:].rearrange("p b n -> p (b n)").bitcast(I32), 0)

from contextlib import ExitStack

import concourse.mybir as mybir
from concourse.masks import make_identity

K, T, S, V, H, N = 512, 4096, 1024, 512, 512, 128
FLOPS = 2 * K * H * S + 2 * 2 * H * N * V

F32 = mybir.dt.float32
BF16 = mybir.dt.bfloat16
I32 = mybir.dt.int32
U32 = mybir.dt.uint32
U16 = mybir.dt.uint16
U8 = mybir.dt.uint8
FP8X4 = mybir.dt.float8_e4m3fn_x4
FP4X4 = mybir.dt.float4_e2m1fn_x4
ALU = mybir.AluOpType
ACT = mybir.ActivationFunctionType

P = 128
PACK = 4
CH = 128
NCH = V // CH
SM = 56
WARM_WIDTHS = (256, 512, 512)
GP = 72
CUT = T // 2


def tile_picked_haar_relu_p_kernel(
    tc, x_words, x_scales, w1, w2_words, w2_scales, w3_words, w3_scales, offs, out
):
    nc = tc.nc
    with ExitStack() as ctx:
        keep = ctx.enter_context(tc.tile_pool(name="keep", bufs=1))
        psum = ctx.enter_context(tc.psum_pool(name="psum", bufs=1))

        reuse = ctx.enter_context(tc.tile_pool(name="reuse", bufs=1))

        w1_raw = keep.tile([P, PACK, H], F32, name="w1_raw", align_bytes=64)
        nc.sync.dma_start(w1_raw[:], w1.rearrange("(p j) c -> p j c", j=PACK))
        offsets = keep.tile([P, S // 16], U16, name="offsets")
        nc.sync.dma_start(offsets[:], offs)

        xs_all = reuse.tile([P, T], U8, name="xs_all", offset=0, align_bytes=64)
        nc.vector.memset(xs_all[:].bitcast(I32), 0)
        nc.sync.dma_start(xs_all[32:96:4, :].bitcast(I32), x_scales[0].bitcast(I32))

        xs = keep.tile([P, S], U8, name="xs", align_bytes=64)
        zeros = reuse.tile([P, S // 4], I32, name="zeros", offset=24576 - 512, align_bytes=64)
        nc.vector.memset(zeros[:], 0)
        nc.vector.tensor_copy(xs[:].bitcast(I32), zeros[:])
        xw_all = reuse.tile([P, T], I32, name="xw_all", offset=8192, align_bytes=64)
        words_in = x_words[0].rearrange("p c r -> p (c r)").bitcast(I32)
        nc.scalar.dma_start(xw_all[:, CUT:], words_in[:, CUT:])
        nc.sync.dma_start(xw_all[:, :CUT], words_in[:, :CUT])
        w2_sb = reuse.tile([P, 2 * N], U8, name="w2_sb", offset=1536, align_bytes=64)

        xs_spread = keep.tile([P, S], U8, name="xs_spread", align_bytes=64)
        nc.vector.tensor_copy(xs_spread[:], xs_all[:].indirect(offsets[:]))
        for r in range(4):
            nc.sync.dma_start(xs[r:P:32, :].bitcast(I32), xs_spread[32 + 4 * r : 96 : 16, :].bitcast(I32))

        w3_sb = reuse.tile([P, 2 * N], U8, name="w3_sb", offset=512, align_bytes=64)
        wb_words = (w2_sb, w3_sb)
        nc.sync.dma_start(w2_sb[:].bitcast(I32), w2_words[0].bitcast(I32))
        nc.sync.dma_start(w3_sb[:].bitcast(I32), w3_words[0].bitcast(I32))

        w1_bf = keep.tile([P, PACK * H], BF16, name="w1_bf", align_bytes=64)
        cast_out = w1_bf[:].rearrange("p (t m j) -> p m t j", t=PACK, j=PACK)
        cast_in = w1_raw[:].rearrange("p j (m t) -> p m t j", t=PACK)
        nc.scalar.copy(cast_out[:, :SM], cast_in[:, :SM])
        for t0 in (0, 2):
            nc.vector.tensor_copy(cast_out[:, SM:, t0 : t0 + 2], cast_in[:, SM:, t0 : t0 + 2])
        w1_codes = keep.tile([P, H], U32, name="w1_codes", align_bytes=64)
        w1_scales = reuse.tile([P, H], U8, name="w1_scales", offset=0, align_bytes=64)
        for t0 in (0, 2):
            cols = slice(t0 * P, (t0 + 2) * P)
            nc.vector.quantize_mx(out=w1_codes[:, cols].bitcast(FP8X4), scales=w1_scales[:, cols], in_=w1_bf[:, t0 * H : (t0 + 2) * H])

        wb_scales = reuse.tile([P, 2, N], U8, name="wb_scales", offset=1024, align_bytes=64)
        nc.vector.memset(wb_scales[:].rearrange("p b n -> p (b n)").bitcast(I32), 0)
        for b, scales in ((1, w3_scales), (0, w2_scales)):
            rows = scales[0].rearrange("(q r) c -> r q c", r=4)
            for r in range(4):
                nc.sync.dma_start(wb_scales[r:P:32, b, :].bitcast(I32), rows[r].bitcast(I32))

        for i, width in enumerate(WARM_WIDTHS):
            warm = psum.tile([P, H], F32, name=f"warm{i}", tag=f"bank{5 + i}")
            nc.tensor.matmul_mx(
                out=warm[:, :width],
                lhsT=w1_codes[:, :P].bitcast(FP8X4),
                lhsT_scale=w1_scales[:, :P],
                rhs=w1_codes[:, :width].bitcast(FP8X4),
                rhs_scale=w1_scales[:, :width],
                start=True,
                stop=True,
            )

        xw = [keep.tile([P, V], U32, name=f"xw{d}", align_bytes=64) for d in range(2)]
        for d in (1, 0):
            nc.vector.tensor_copy(xw[d][:], xw_all[:].bitcast(U32).indirect(offsets[:, d * V // 16 : (d + 1) * V // 16]))

        identity = keep.tile([P, P], F32, name="identity", align_bytes=64)
        make_identity(nc, identity[:])

        def turned_product(d, c, bank):
            acc = psum.tile([CH, H], F32, name=f"ht{d}_{c}", tag=f"bank{bank}")
            nc.tensor.matmul_mx(
                out=acc[:],
                lhsT=xw[d][:, c * CH : (c + 1) * CH].bitcast(FP8X4),
                lhsT_scale=xs[:, d * V + c * CH : d * V + (c + 1) * CH],
                rhs=w1_codes[:].bitcast(FP8X4),
                rhs_scale=w1_scales[:],
                start=True,
                stop=True,
            )
            return acc

        def first_product(d, c, bank):
            acc = psum.tile([P, PACK, CH], F32, name=f"h{d}_{c}", tag=f"bank{bank}")
            for t in range(PACK):
                nc.tensor.matmul_mx(
                    out=acc[:, t, :],
                    lhsT=w1_codes[:, t * P : (t + 1) * P].bitcast(FP8X4),
                    lhsT_scale=w1_scales[:, t * P : (t + 1) * P],
                    rhs=xw[d][:, c * CH : (c + 1) * CH].bitcast(FP8X4),
                    rhs_scale=xs[:, d * V + c * CH : d * V + (c + 1) * CH],
                    start=True,
                    stop=True,
                )
            return acc[:].rearrange("p t v -> p v t")

        bands = [keep.tile([P, 2, CH, PACK], BF16, name=f"bands{c}", align_bytes=64) for c in range(NCH)]
        h0_sb = reuse.tile([P, GP, PACK], F32, name="h0_sb", offset=2048, align_bytes=64)
        h1 = {c: keep.tile([P, CH, PACK], F32, name=f"h1_{c}", align_bytes=64) for c in (0, 1, 3)}

        def both_bands(c, v0):
            for b, op in enumerate((ALU.add, ALU.subtract)):
                nc.vector.scalar_tensor_tensor(bands[c][:, b, v0:], pre0[c][:, v0:], 0.0, h1[c][:, v0:], ALU.max, op)

        pre1 = {0: first_product(1, 0, 0)}
        pre_t1 = turned_product(1, 2, 1)
        pre1[3] = first_product(1, 3, 2)
        pre0 = {0: first_product(0, 0, 3), 3: first_product(0, 3, 4)}
        pre1[1] = first_product(1, 1, 5)
        pre_t0 = turned_product(0, 2, 6)
        pre0[1] = first_product(0, 1, 7)

        ht = [keep.tile([CH, H], F32, name=f"ht_sb{i}", align_bytes=64) for i in range(3)]
        nc.scalar.activation(h1[0][:], pre1[0], ACT.Relu)
        nc.vector.tensor_scalar_max(ht[1][:], pre_t1[:], 0.0)
        nc.gpsimd.tensor_scalar(ht[2][:], ht[1][:], -1.0, 0.0, ALU.mult, ALU.add)
        nc.scalar.activation(h1[3][:], pre1[3], ACT.Relu)
        both_bands(0, 0)
        nc.scalar.activation(h0_sb[:], pre0[3][:, :GP], ACT.Relu)
        for b, op in enumerate((ALU.add, ALU.subtract)):
            nc.gpsimd.tensor_tensor(bands[3][:, b, :GP], h0_sb[:], h1[3][:, :GP], op)
        both_bands(3, GP)
        nc.scalar.activation(h1[1][:], pre1[1], ACT.Relu)
        both_bands(1, 0)
        for half in range(2):
            cols = slice(half * H // 2, (half + 1) * H // 2)
            nc.scalar.activation(ht[0][:, cols], pre_t0[:, cols], ACT.Relu)
        turned = [psum.tile([P, PACK, CH], F32, name=f"turned{b}", tag=f"bank{b}") for b in range(2)]
        for b in range(2):
            for t in range(PACK):
                nc.tensor.matmul(turned[b][:, t, :], ht[1 + b][:, t * P : (t + 1) * P], identity[:], start=(t == 0), stop=False, is_transpose=True)
        for t0 in (0, 2):
            for b in range(2):
                for t in (t0, t0 + 1):
                    nc.tensor.matmul(turned[b][:, t, :], ht[0][:, t * P : (t + 1) * P], identity[:], start=False, stop=(t == PACK - 1), is_transpose=True)
        for b in range(2):
            nc.scalar.copy(bands[2][:, b], turned[b][:].rearrange("p t v -> p v t"))

        codes = {0: reuse.tile([P, 2 * CH], U32, name="codes0", offset=2048, align_bytes=64)}
        for c in (1, 2, 3):
            codes[c] = keep.tile([P, 2 * CH], U32, name=f"codes{c}", align_bytes=64)
        for c in (0, 1, 3, 2):
            bscales = keep.tile([P, 2 * CH], U8, name=f"bscales{c}", align_bytes=64)
            for b in range(2):
                nc.vector.quantize_mx(
                    out=codes[c][:, b * CH : (b + 1) * CH].bitcast(FP8X4),
                    scales=bscales[:, b * CH : (b + 1) * CH],
                    in_=bands[c][:, b].rearrange("p v t -> p (v t)"),
                )
            acc = psum.tile([N, CH], F32, name=f"o{c}", tag=f"bank{(2, 3, 6, 5)[c]}")
            for b in range(2):
                nc.tensor.matmul_mx(
                    out=acc[:],
                    lhsT=wb_words[b][:].bitcast(FP4X4),
                    lhsT_scale=wb_scales[:, b, :],
                    rhs=codes[c][:, b * CH : (b + 1) * CH].bitcast(FP8X4),
                    rhs_scale=bscales[:, b * CH : (b + 1) * CH],
                    start=(b == 0),
                    stop=(b == 1),
                )
            res = keep.tile([N, CH], F32, name=f"res{c}")
            nc.scalar.activation(res[:], acc[:], ACT.Copy, scale=0.5)
            nc.sync.dma_start(out[:, c * CH : (c + 1) * CH], res[:])
